import numpy as np
import ml_dtypes


def mxq(x, axis, fmt="e4m3"):
    dtype, down = {"e4m3": (ml_dtypes.float8_e4m3fn, 7), "e5m2": (ml_dtypes.float8_e5m2, 14)}[fmt]
    v = np.moveaxis(np.asarray(x, np.float32).astype(ml_dtypes.bfloat16).astype(np.float64), axis, -1)
    blocks = v.reshape(v.shape[:-1] + (-1, 32))
    amax = np.abs(blocks).max(-1, keepdims=True)
    byte = np.maximum(np.where(amax > 0, np.frexp(amax)[1] - 1 + 127, 0) - down, 1)
    scale = np.exp2(byte - 127.0)
    codes = (blocks / scale).astype(np.float32).astype(dtype).astype(np.float64)
    return np.moveaxis((codes * scale).reshape(v.shape), -1, axis)


WIDE = False


def mx_kscale(k):
    if not WIDE:
        return np.ones(k)
    levels = np.array([10, -10, 5, -5, 0])
    if k % 512:
        return np.exp2(np.random.permutation(np.resize(levels, k // 32))).repeat(32)
    a = np.empty((k // 512, 16))
    for p in range(k // 512):
        a[p, :8] = np.random.permutation(np.resize(levels, 8))
        for g in range(8):
            far = levels[np.abs(levels - a[p, g]) >= 10]
            a[p, g + 8] = far[np.random.randint(len(far))]
    return np.exp2(a.ravel()).repeat(32)


def f64(x):
    return np.asarray(x).astype(np.float64)


def striped(idx):
    return np.tile(idx.reshape(-1, 16).T, (8, 1)).astype(np.uint16)


def unstriped(offs):
    return offs[:16].T.reshape(-1).astype(np.int64)


def striped8(idx):
    return np.concatenate([x.reshape(-1, 16).T for x in idx]).astype(np.uint16)


def runs(offs, k):
    lists = np.stack([offs[16 * r : 16 * r + 16].T.reshape(-1) for r in range(8)]).astype(np.int64)
    return lists[np.arange(k) % 512 // 64]


def pack_weight(w):
    k, n = w.shape
    w = f64(np.asarray(w, np.float32).astype(ml_dtypes.bfloat16)).reshape(k // 32, 32, n)
    amax = np.abs(w).max(1)
    byte = np.clip(np.where(amax > 0, np.frexp(amax)[1] - 1 + 127 - 7, 1), 1, 254)
    scaled = (w * np.exp2(127.0 - byte)[:, None, :]).reshape(k, n).astype(np.float32)
    words = np.ascontiguousarray(scaled.reshape(k // 512, 128, 4, n).transpose(0, 1, 3, 2)).astype(ml_dtypes.float8_e4m3fn).view(np.uint8)
    return words, np.ascontiguousarray(byte.astype(np.uint8).reshape(k // 512, 16, n))


def unpack_weight(words, scales):
    g, p, n, _ = words.shape
    vals = np.ascontiguousarray(words).view(ml_dtypes.float8_e4m3fn).astype(np.float64) * np.repeat(np.exp2(scales.astype(np.float64) - 127.0), 8, axis=1)[..., None]
    return vals.transpose(0, 1, 3, 2).reshape(g * 512, n)

def planes(y):
    n, m = y.shape
    v = y.astype(np.float32).astype(ml_dtypes.bfloat16).astype(np.float64).reshape(n // 32, 32, m)
    top = np.abs(v).max(1)
    byte = np.clip(np.where(top > 0, np.frexp(top)[1] - 1 + 127 - 7, 1), 1, 254)
    codes = (v * np.exp2(127.0 - byte)[:, None, :]).reshape(n, m).astype(np.float32).astype(ml_dtypes.float8_e4m3fn).view(np.uint8)
    words = codes.reshape(n // 512, 128, 4, m).transpose(0, 1, 3, 2)
    return np.ascontiguousarray(words), np.ascontiguousarray(byte.astype(np.uint8).reshape(n // 512, 16, m))


K, T, S, N, G, H, J, W = 512, 1024, 512, 512, 2048, 512, 512, 256


def setup_inputs():
    n = np.random.standard_normal
    s = mx_kscale(K)[:, None]
    u = mx_kscale(S)
    packed_xT = pack_weight(n((K, T)) * s)
    packed_dT = pack_weight(n((K, G)) / s)
    packed_w1 = pack_weight(n((H, N)) / np.sqrt(2 * H) / u[:, None])
    packed_w2 = pack_weight(n((H, N)) / np.sqrt(2 * H) / u[:, None])
    perm = np.stack([np.random.permutation(S) for _ in range(8)])
    return {
        "x_words": packed_xT[0],
        "x_scales": packed_xT[1],
        "d_words": packed_dT[0],
        "d_scales": packed_dT[1],
        "tab": n((H, J)).astype(np.float32),
        "gn": (np.random.uniform(0.5, 1.5, (H, 1)) * u[:, None]).astype(np.float32),
        "gm": (np.random.uniform(0.5, 1.5, (H, 1)) * u[:, None]).astype(np.float32),
        "w1_words": packed_w1[0],
        "w1_scales": packed_w1[1],
        "w2_words": packed_w2[0],
        "w2_scales": packed_w2[1],
        "offs": striped(np.random.permutation(T)[:S]),
        "k1": striped8(np.random.randint(0, G, (8, H))),
        "two": striped(np.random.permutation(T)[:S]),
        "k2": striped8(np.random.randint(0, G, (8, H))),
        "n1": striped8(np.random.randint(0, J, (8, S))),
        "n2": striped8(np.stack([np.random.permutation(S) for _ in range(8)])),
        "n3": striped8(np.stack([np.random.permutation(S) for _ in range(8)])),
        "n4": striped8(np.stack([np.random.permutation(S) for _ in range(8)])),
        "n5": striped8(perm[:, :W]),
        "n6": striped8(perm[:, W:]),
    }


def reference(x_words, x_scales, d_words, d_scales, tab, gn, gm, w1_words, w1_scales, w2_words, w2_scales, offs, k1, two, k2, n1, n2, n3, n4, n5, n6):
    d_k1 = unpack_weight(d_words, d_scales)[np.arange(K)[:, None], runs(k1, K)]
    xq = unpack_weight(x_words, x_scales)[:, unstriped(offs)]
    a = 0.0625 * (d_k1.T @ xq)
    z = f64(gn) * (np.maximum(a + f64(tab)[np.arange(H)[:, None], runs(n1, H)], a[np.arange(H)[:, None], runs(n2, H)]))
    d_k2 = unpack_weight(d_words, d_scales)[np.arange(K)[:, None], runs(k2, K)]
    x_two = unpack_weight(x_words, x_scales)[:, unstriped(two)]
    b = 0.0625 * (d_k2.T @ x_two)
    sq = (b) ** 2
    z2 = f64(gm) * ((b[np.arange(H)[:, None], runs(n4, H)]) / (np.sqrt(sq + sq[np.arange(H)[:, None], runs(n3, H)] + 0.25)))
    h = unpack_weight(w1_words, w1_scales).T @ mxq(z, 0, "e4m3") + unpack_weight(w2_words, w2_scales).T @ mxq(z2, 0, "e4m3")
    pa = h[np.arange(N)[:, None], runs(n5, N)]
    pb = h[np.arange(N)[:, None], runs(n6, N)]
    rb = np.maximum(pa, pb)
    ra = pa / (np.abs(pb) + 0.5)
    ds = np.zeros((N, S))
    ds[np.arange(N)[:, None], runs(n5, N)] = ra
    out = ds.copy()
    out[np.arange(N)[:, None], runs(n6, N)] = rb
    return (out,) + planes(out)

@@ -1,0 +1,251 @@
+from contextlib import ExitStack
+
+import concourse.mybir as mybir
+
+K, T, S, N, G, H, J, W = 512, 1024, 512, 512, 2048, 512, 512, 256
+FLOPS = 4 * 2 * 512 * 512 * 512
+
+F32 = mybir.dt.float32
+BF16 = mybir.dt.bfloat16
+I32 = mybir.dt.int32
+U32 = mybir.dt.uint32
+U16 = mybir.dt.uint16
+U8 = mybir.dt.uint8
+FP8X4 = mybir.dt.float8_e4m3fn_x4
+ACT = mybir.ActivationFunctionType
+ALU = mybir.AluOpType
+
+P = 128
+PACK = 4
+HALF = S // 2
+
+
+def tile_picked_pqjkindrmsratio_none_po_kernel(
+    tc, x_words, x_scales, d_words, d_scales, tab, gn, gm, w1_words, w1_scales, w2_words, w2_scales,
+    offs, k1, two, k2, n1, n2, n3, n4, n5, n6, out_0, out_1, out_2,
+):
+    nc = tc.nc
+    with ExitStack() as ctx:
+        lists = ctx.enter_context(tc.tile_pool(name="lists", bufs=1))
+        sb = ctx.enter_context(tc.tile_pool(name="sb", bufs=1))
+        turns = ctx.enter_context(tc.tile_pool(name="turns", bufs=1))
+        after = ctx.enter_context(tc.tile_pool(name="after", bufs=1))
+        psum = ctx.enter_context(tc.psum_pool(name="psum", bufs=1))
+
+        def tile(name, width, dtype):
+            return sb.tile([P, width], dtype, name=name, align_bytes=64)
+
+        def planes(name, width=S, dtype=F32):
+            return [tile(f"{name}{t}", width, dtype) for t in range(PACK)]
+
+        def load_list(name, src):
+            held = lists.tile(list(src.shape), U16, name=name)
+            nc.sync.dma_start(held[:], src)
+            return held
+
+        def load_words(name, src):
+            held = tile(name, src.shape[2], U32)
+            nc.sync.dma_start(held[:].bitcast(I32), src[0].rearrange("p c r -> p (c r)").bitcast(I32))
+            return held
+
+        def cut(offsets):
+            return [(slice(c * HALF, (c + 1) * HALF), offsets[:, c * HALF // 16 : (c + 1) * HALF // 16]) for c in range(2)]
+
+        def deal(copy, dst, src, run):
+            copy(dst.rearrange("p (t m i) -> p m t i", t=PACK, i=run), src.rearrange("p (m i t) -> p m t i", t=PACK, i=run))
+
+        d_bytes = tile("d_bytes", G, U8)
+        x_bytes = tile("x_bytes", T, U8)
+        picked_scales = [tile("b_scales", H + S, U8), tile("a_scales", H + S, U8)]
+        w_scales = tile("w_scales", 2 * N, U8)
+        nc.gpsimd.memset(d_bytes[:].bitcast(I32), 0)
+        nc.gpsimd.memset(x_bytes[:].bitcast(I32), 0)
+        for held in picked_scales:
+            nc.vector.memset(held[:].bitcast(I32), 0)
+        nc.vector.memset(w_scales[:].bitcast(I32), 0)
+
+        def load_gain(name, src, offset):
+            held = after.tile([P, PACK], F32, name=name, offset=offset, align_bytes=64)
+            nc.sync.dma_start(held[:], src.rearrange("(p t) o -> p (t o)", t=PACK))
+            return held
+
+        nc.sync.dma_start(d_bytes[0:P:8, :].bitcast(I32), d_scales[0].bitcast(I32))
+        nc.sync.dma_start(x_bytes[0:P:8, :].bitcast(I32), x_scales[0].bitcast(I32))
+        k2_l = load_list("k2_l", k2)
+        two_l = load_list("two_l", two)
+        n1_l = load_list("n1_l", n1)
+        k1_l = load_list("k1_l", k1)
+        tab_rows = tab.rearrange("(p t) c -> p t c", t=PACK)
+        tabs = planes("tab")
+        x_w = load_words("x_w", x_words)
+        d_w = load_words("d_w", d_words)
+        offs_l = load_list("offs_l", offs)
+        for t in range(PACK):
+            nc.gpsimd.dma_start(tabs[t][:], tab_rows[:, t, :])
+        n3_l = load_list("n3_l", n3)
+        n4_l = load_list("n4_l", n4)
+        n2_l = load_list("n2_l", n2)
+        n5_l = load_list("n5_l", n5)
+        n6_l = load_list("n6_l", n6)
+
+        sq_win, bg_win, a_win = planes("sq_win", 2 * S), planes("bg_win", 2 * S), planes("a_win", 2 * S)
+        sq, tab_g = [w[:, :S] for w in sq_win], [w[:, S:] for w in sq_win]
+        bg, sq_own = [w[:, :S] for w in bg_win], [w[:, S:] for w in bg_win]
+        a, root = [w[:, :S] for w in a_win], [w[:, S:] for w in a_win]
+        for t in range(PACK):
+            for cols, offsets in cut(n1_l):
+                nc.scalar.activation(tab_g[t][:, cols], tabs[t][:].indirect(offsets), ACT.Copy)
+
+        def first_product(name, l, d_list, x_list, picked):
+            gd, gx, xg, dg, spread = picked
+            nc.vector.tensor_copy(gd, d_bytes[:].indirect(d_list[:]))
+            nc.vector.tensor_copy(gx, x_bytes[:].indirect(x_list[:]))
+            deal(nc.vector.tensor_copy, spread[:, :H], gd, 16)
+            nc.vector.tensor_copy(spread[:, H:].bitcast(I32), gx.bitcast(I32))
+            scales = picked_scales[l]
+            for j in range(4):
+                nc.sync.dma_start(scales[j:P:32, :].bitcast(I32), spread[8 * j : P : 32, :].bitcast(I32))
+            nc.vector.tensor_copy(dg, d_w[:].indirect(d_list[:]))
+            nc.vector.tensor_copy(xg, x_w[:].indirect(x_list[:]))
+            dd = tile(name + "_dd", H, U32)
+            deal(nc.vector.tensor_copy, dd[:].bitcast(I32), dg.bitcast(I32), 4)
+            banks = []
+            for t in range(PACK):
+                bank = psum.tile([P, S], F32, name=f"{name}{t}", tag=f"bank{4 * l + t}")
+                nc.tensor.matmul_mx(
+                    out=bank[:],
+                    lhsT=dd[:, t * P : (t + 1) * P].bitcast(FP8X4),
+                    lhsT_scale=scales[:, t * P : (t + 1) * P],
+                    rhs=xg.bitcast(FP8X4),
+                    rhs_scale=scales[:, H:],
+                    start=True,
+                    stop=True,
+                )
+                banks.append(bank)
+            return banks
+
+        b_gd = tile("b_gd", H, U8)
+        b_spread = after.tile([P, H + S], U8, name="b_spread", offset=4 * N - H, align_bytes=64)
+        b_gx = after.tile([P, S], U8, name="b_gx", offset=10 * N, align_bytes=64)
+        b_xg = tile("b_xg", S, U32)
+        b_dg = turns.tile([P, H], U32, name="b_dg", offset=0, align_bytes=64)
+        b_banks = first_product("b", 0, k2_l, two_l, (b_gd[:], b_gx[:], b_xg[:], b_dg[:], b_spread))
+        gm_t = load_gain("gm_t", gm, 10 * N)
+        a_bytes = turns.tile([P, H + S], U8, name="a_bytes", offset=0, align_bytes=64)
+        a_words = turns.tile([P, S + H], U32, name="a_words", offset=H + S, align_bytes=64)
+        a_banks = first_product("a", 1, k1_l, offs_l, (a_bytes[:, :H], a_bytes[:, H:], a_words[:, :S], a_words[:, S:], tile("a_spread", H + S, U8)))
+
+        w_raw = []
+        for l, src in enumerate((w1_words, w2_words)):
+            held = after.tile([P, N], U32, name=f"w_raw{l}", offset=l * 4 * N, align_bytes=64)
+            nc.sync.dma_start(held[:].bitcast(I32), src[0].rearrange("p c r -> p (c r)").bitcast(I32))
+            w_raw.append(held)
+        gn_t = load_gain("gn_t", gn, 10 * N + 64)
+        w_bytes = after.tile([P, 2 * N], U8, name="w_bytes", offset=10 * N + 128, align_bytes=64)
+        nc.gpsimd.memset(w_bytes[:].bitcast(I32), 0)
+        for l, src in enumerate((w1_scales, w2_scales)):
+            nc.sync.dma_start(w_bytes[0:P:8, l * N : (l + 1) * N].bitcast(I32), src[0].bitcast(I32))
+        w_spread = tile("w_spread", 2 * N, U8)
+        for l in range(2):
+            deal(nc.gpsimd.tensor_copy, w_spread[:, l * N : (l + 1) * N], w_bytes[:, l * N : (l + 1) * N], 16)
+        for j in range(4):
+            nc.sync.dma_start(w_scales[j:P:32, :].bitcast(I32), w_spread[8 * j : P : 32, :].bitcast(I32))
+
+        under, u, v, top = planes("under"), planes("u"), planes("v"), planes("top")
+        z2 = tile("z2", PACK * S, F32)
+        z = tile("z", PACK * S, BF16)
+        for t in range(PACK):
+            nc.scalar.activation(sq[t], b_banks[t][:], ACT.Square, scale=0.0625)
+            nc.gpsimd.tensor_scalar(sq_own[t], sq[t], 1.0, 0.0, ALU.mult, ALU.add)
+        for t in range(PACK):
+            nc.scalar.activation(bg[t], b_banks[t][:], ACT.Copy, scale=gm_t[:, t : t + 1])
+        w_words = []
+        for l in range(2):
+            held = tile(f"w_words{l}", N, U32)
+            deal(nc.scalar.copy, held[:], w_raw[l][:], 4)
+            w_words.append(held)
+        for t in range(PACK):
+            nc.vector.tensor_tensor(under[t][:], sq_win[t][:].indirect(n3_l[:]), sq_own[t], ALU.add)
+        for t in range(PACK):
+            nc.scalar.activation(a[t], a_banks[t][:], ACT.Copy, scale=0.0625)
+        for t in range(PACK):
+            nc.vector.scalar_tensor_tensor(u[t][:], a_banks[t][:], 0.0625, tab_g[t], ALU.mult, ALU.add)
+        for t in range(PACK):
+            nc.scalar.activation(root[t], under[t][:], ACT.Abs_reciprocal_sqrt, bias=64.0, scale=256.0)
+        for t in range(PACK):
+            nc.vector.tensor_tensor(z2[:, t * S : (t + 1) * S], bg_win[t][:].indirect(n4_l[:]), root[t], ALU.mult)
+        for t in range(PACK):
+            nc.scalar.activation(v[t][:], a_win[t][:].indirect(n2_l[:]), ACT.Copy)
+
+        def quantise(name, src, scalar_cols):
+            grouped = tile(name + "_grouped", PACK * S, BF16)
+            dst = grouped[:].rearrange("p (c i t) -> p c t i", i=4, t=PACK)
+            rows = src[:].rearrange("p (t c i) -> p c t i", i=4, t=PACK)
+            cut_at = scalar_cols // 4
+            if cut_at:
+                nc.scalar.copy(dst[:, :cut_at], rows[:, :cut_at])
+            nc.vector.tensor_copy(dst[:, cut_at:], rows[:, cut_at:])
+            words = tile(name + "_words", S, U32)
+            scales = tile(name + "_scales", S, U8)
+            nc.vector.quantize_mx(out=words[:].bitcast(FP8X4), scales=scales[:], in_=grouped[:])
+            return words, scales
+
+        for t in range(PACK):
+            nc.vector.tensor_tensor(top[t][:], u[t][:], v[t][:], ALU.max)
+        z2_q = quantise("z2", z2, 256)
+        for t in range(PACK):
+            nc.scalar.activation(z[:, t * S : (t + 1) * S], top[t][:], ACT.Copy, scale=gn_t[:, t : t + 1])
+        z_q = quantise("z", z, 128)
+
+        h_banks = [psum.tile([P, S], F32, name=f"h{t}", tag=f"bank{t}") for t in range(PACK)]
+        for l, (words, scales) in ((1, z2_q), (0, z_q)):
+            for t in range(PACK):
+                nc.tensor.matmul_mx(
+                    out=h_banks[t][:],
+                    lhsT=w_words[l][:, t * P : (t + 1) * P].bitcast(FP8X4),
+                    lhsT_scale=w_scales[:, l * N + t * P : l * N + (t + 1) * P],
+                    rhs=words[:].bitcast(FP8X4),
+                    rhs_scale=scales[:],
+                    start=(l == 1),
+                    stop=(l == 0),
+                )
+
+        y = planes("y")
+        pa, pb, rb = planes("pa", W), planes("pb", W), planes("rb", W)
+        size, inverse = planes("size", W), planes("inverse", W)
+        size_sq_all = sb.tile([P, PACK * W], F32, name="size_sq_all", tag="late", align_bytes=64)
+        size_sq = [size_sq_all[:, t * W : (t + 1) * W] for t in range(PACK)]
+        out_rows = out_0.rearrange("(p t) c -> p t c", t=PACK)
+
+        def fetch(t):
+            h = sb.tile([P, S], F32, name="h", tag=f"h{t // 2}", align_bytes=64)
+            nc.scalar.activation(h[:], h_banks[t][:], ACT.Copy)
+            for dst, offsets in ((pb[t], n6_l), (pa[t], n5_l)):
+                if t == 0 and dst is pb[t]:
+                    nc.vector.tensor_copy(dst[:], h[:].indirect(offsets[:]))
+                else:
+                    nc.scalar.activation(dst[:], h[:].indirect(offsets[:]), ACT.Copy)
+            nc.vector.tensor_tensor(rb[t][:], pa[t][:], pb[t][:], ALU.max)
+
+        fetch(0)
+        for t in range(PACK):
+            nc.vector.tensor_copy(y[t][:].indirect(n6_l[:]), rb[t][:])
+            if t + 1 < PACK:
+                fetch(t + 1)
+            nc.scalar.activation(size[t][:], pb[t][:], ACT.Abs)
+            nc.scalar.activation(size_sq[t], size[t][:], ACT.Square, bias=0.5)
+            nc.scalar.activation(inverse[t][:], size_sq[t], ACT.Abs_reciprocal_sqrt)
+            nc.vector.tensor_tensor(y[t][:].indirect(n5_l[:]), pa[t][:], inverse[t][:], ALU.mult)
+            nc.sync.dma_start(out_rows[:, t, :], y[t][:])
+        y_bf = sb.tile([P, PACK * S], BF16, name="y_bf", tag="late", align_bytes=64)
+        for t in range(PACK):
+            if t < PACK - 1:
+                nc.scalar.copy(y_bf[:, t * S : (t + 1) * S], y[t][:])
+            else:
+                nc.vector.tensor_copy(y_bf[:, t * S : (t + 1) * S], y[t][:])
+
+        y_words, y_scales = quantise("y", y_bf, 128)
+        nc.sync.dma_start(out_1[0].rearrange("p c r -> p (c r)").bitcast(I32), y_words[:].bitcast(I32))
+        for q in range(4):
+            queue = nc.sync if q % 2 else nc.scalar
+            queue.dma_start(out_2[0, 4 * q : 4 * q + 4, :].bitcast(I32), y_scales[32 * q : 32 * q + 4, :].bitcast(I32))

@@ -64,6 +64,11 @@ def tile_picked_pqjkindrmsratio_none_po_kernel(
             nc.vector.memset(held[:].bitcast(I32), 0)
         nc.vector.memset(w_scales[:].bitcast(I32), 0)
 
+        warm_in = sb.tile([P, 1], F32, name="warm_in")
+        warm_out = sb.tile([P, 1], F32, name="warm_out")
+        nc.vector.memset(warm_in[:], 1.0)
+        nc.scalar.activation(warm_out[:], warm_in[:], ACT.Abs_reciprocal_sqrt)
+
         def load_gain(name, src, offset):
             held = after.tile([P, PACK], F32, name=name, offset=offset, align_bytes=64)
             nc.sync.dma_start(held[:], src.rearrange("(p t) o -> p (t o)", t=PACK))

@@ -63,6 +63,8 @@ def tile_picked_pqjkindrmsratio_none_po_kernel(
         for held in picked_scales:
             nc.vector.memset(held[:].bitcast(I32), 0)
         nc.vector.memset(w_scales[:].bitcast(I32), 0)
+        w_bytes = tile("w_bytes", 2 * N, U8)
+        nc.vector.memset(w_bytes[:].bitcast(I32), 0)
 
         warm_in = sb.tile([P, 1], F32, name="warm_in")
         warm_out = sb.tile([P, 1], F32, name="warm_out")
@@ -84,14 +86,17 @@ def tile_picked_pqjkindrmsratio_none_po_kernel(
         tabs = planes("tab")
         x_w = load_words("x_w", x_words)
         d_w = load_words("d_w", d_words)
+        nc.sync.dma_start(tabs[0][:], tab_rows[:, 0, :])
         offs_l = load_list("offs_l", offs)
-        for t in range(PACK):
-            nc.gpsimd.dma_start(tabs[t][:], tab_rows[:, t, :])
         n3_l = load_list("n3_l", n3)
         n4_l = load_list("n4_l", n4)
         n2_l = load_list("n2_l", n2)
+        for t in range(1, PACK):
+            nc.sync.dma_start(tabs[t][:], tab_rows[:, t, :])
         n5_l = load_list("n5_l", n5)
         n6_l = load_list("n6_l", n6)
+        for l, src in enumerate((w1_scales, w2_scales)):
+            nc.gpsimd.dma_start(w_bytes[0:P:8, l * N : (l + 1) * N].bitcast(I32), src[0].bitcast(I32))
 
         sq_win, bg_win, a_win = planes("sq_win", 2 * S), planes("bg_win", 2 * S), planes("a_win", 2 * S)
         sq, tab_g = [w[:, :S] for w in sq_win], [w[:, S:] for w in sq_win]
@@ -146,13 +151,9 @@ def tile_picked_pqjkindrmsratio_none_po_kernel(
             nc.sync.dma_start(held[:].bitcast(I32), src[0].rearrange("p c r -> p (c r)").bitcast(I32))
             w_raw.append(held)
         gn_t = load_gain("gn_t", gn, 10 * N + 64)
-        w_bytes = after.tile([P, 2 * N], U8, name="w_bytes", offset=10 * N + 128, align_bytes=64)
-        nc.gpsimd.memset(w_bytes[:].bitcast(I32), 0)
-        for l, src in enumerate((w1_scales, w2_scales)):
-            nc.sync.dma_start(w_bytes[0:P:8, l * N : (l + 1) * N].bitcast(I32), src[0].bitcast(I32))
-        w_spread = tile("w_spread", 2 * N, U8)
+        w_spread = turns.tile([P, 2 * N], U8, name="w_spread", offset=H + S, align_bytes=64)
         for l in range(2):
-            deal(nc.gpsimd.tensor_copy, w_spread[:, l * N : (l + 1) * N], w_bytes[:, l * N : (l + 1) * N], 16)
+            deal(nc.vector.tensor_copy, w_spread[:, l * N : (l + 1) * N], w_bytes[:, l * N : (l + 1) * N], 16)
         for j in range(4):
             nc.sync.dma_start(w_scales[j:P:32, :].bitcast(I32), w_spread[8 * j : P : 32, :].bitcast(I32))
 
@@ -161,14 +162,9 @@ def tile_picked_pqjkindrmsratio_none_po_kernel(
         z = tile("z", PACK * S, BF16)
         for t in range(PACK):
             nc.scalar.activation(sq[t], b_banks[t][:], ACT.Square, scale=0.0625)
-            nc.gpsimd.tensor_scalar(sq_own[t], sq[t], 1.0, 0.0, ALU.mult, ALU.add)
+            nc.scalar.activation(sq_own[t], b_banks[t][:], ACT.Square, scale=0.0625)
         for t in range(PACK):
             nc.scalar.activation(bg[t], b_banks[t][:], ACT.Copy, scale=gm_t[:, t : t + 1])
-        w_words = []
-        for l in range(2):
-            held = tile(f"w_words{l}", N, U32)
-            deal(nc.scalar.copy, held[:], w_raw[l][:], 4)
-            w_words.append(held)
         for t in range(PACK):
             nc.vector.tensor_tensor(under[t][:], sq_win[t][:].indirect(n3_l[:]), sq_own[t], ALU.add)
         for t in range(PACK):
@@ -181,6 +177,11 @@ def tile_picked_pqjkindrmsratio_none_po_kernel(
             nc.vector.tensor_tensor(z2[:, t * S : (t + 1) * S], bg_win[t][:].indirect(n4_l[:]), root[t], ALU.mult)
         for t in range(PACK):
             nc.scalar.activation(v[t][:], a_win[t][:].indirect(n2_l[:]), ACT.Copy)
+        w_words = []
+        for l in range(2):
+            held = sb.tile([P, N], U32, name=f"w_words{l}", tag=f"under{l + 2}", align_bytes=64)
+            deal(nc.scalar.copy, held[:], w_raw[l][:], 4)
+            w_words.append(held)
 
         def quantise(name, src, scalar_cols):
             grouped = tile(name + "_grouped", PACK * S, BF16)
@@ -197,10 +198,10 @@ def tile_picked_pqjkindrmsratio_none_po_kernel(
 
         for t in range(PACK):
             nc.vector.tensor_tensor(top[t][:], u[t][:], v[t][:], ALU.max)
-        z2_q = quantise("z2", z2, 256)
+        z2_q = quantise("z2", z2, 0)
         for t in range(PACK):
             nc.scalar.activation(z[:, t * S : (t + 1) * S], top[t][:], ACT.Copy, scale=gn_t[:, t : t + 1])
-        z_q = quantise("z", z, 128)
+        z_q = quantise("z", z, 256)
 
         h_banks = [psum.tile([P, S], F32, name=f"h{t}", tag=f"bank{t}") for t in range(PACK)]
         for l, (words, scales) in ((1, z2_q), (0, z_q)):
@@ -223,10 +224,10 @@ def tile_picked_pqjkindrmsratio_none_po_kernel(
         out_rows = out_0.rearrange("(p t) c -> p t c", t=PACK)
 
         def fetch(t):
-            h = sb.tile([P, S], F32, name="h", tag=f"h{t // 2}", align_bytes=64)
+            h = sb.tile([P, S], F32, name="h", tag=f"h{min(t, 1)}", align_bytes=64)
             nc.scalar.activation(h[:], h_banks[t][:], ACT.Copy)
             for dst, offsets in ((pb[t], n6_l), (pa[t], n5_l)):
-                if t == 0 and dst is pb[t]:
+                if t == 0:
                     nc.vector.tensor_copy(dst[:], h[:].indirect(offsets[:]))
                 else:
                     nc.scalar.activation(dst[:], h[:].indirect(offsets[:]), ACT.Copy)

@@ -18,6 +18,7 @@ ALU = mybir.AluOpType
 P = 128
 PACK = 4
 HALF = S // 2
+SCALAR_COLS = 128
 
 
 def tile_picked_pqjkindrmsratio_none_po_kernel(
@@ -43,8 +44,7 @@ def tile_picked_pqjkindrmsratio_none_po_kernel(
             nc.sync.dma_start(held[:], src)
             return held
 
-        def load_words(name, src):
-            held = tile(name, src.shape[2], U32)
+        def load_words(held, src):
             nc.sync.dma_start(held[:].bitcast(I32), src[0].rearrange("p c r -> p (c r)").bitcast(I32))
             return held
 
@@ -84,24 +84,21 @@ def tile_picked_pqjkindrmsratio_none_po_kernel(
         k1_l = load_list("k1_l", k1)
         tab_rows = tab.rearrange("(p t) c -> p t c", t=PACK)
         tabs = planes("tab")
-        x_w = load_words("x_w", x_words)
-        d_w = load_words("d_w", d_words)
-        nc.sync.dma_start(tabs[0][:], tab_rows[:, 0, :])
-        offs_l = load_list("offs_l", offs)
-        n3_l = load_list("n3_l", n3)
-        n4_l = load_list("n4_l", n4)
-        n2_l = load_list("n2_l", n2)
-        for t in range(1, PACK):
+        for t in range(2):
             nc.sync.dma_start(tabs[t][:], tab_rows[:, t, :])
-        n5_l = load_list("n5_l", n5)
-        n6_l = load_list("n6_l", n6)
+        x_w = load_words(tile("x_w", T, U32), x_words)
+        d_w = load_words(tile("d_w", G, U32), d_words)
+        offs_l = load_list("offs_l", offs)
+        for t in range(2, PACK):
+            nc.sync.dma_start(tabs[t][:], tab_rows[:, t, :])
+        n3_l = load_list("n3_l", n3)
         for l, src in enumerate((w1_scales, w2_scales)):
             nc.gpsimd.dma_start(w_bytes[0:P:8, l * N : (l + 1) * N].bitcast(I32), src[0].bitcast(I32))
 
         sq_win, bg_win, a_win = planes("sq_win", 2 * S), planes("bg_win", 2 * S), planes("a_win", 2 * S)
         sq, tab_g = [w[:, :S] for w in sq_win], [w[:, S:] for w in sq_win]
-        bg, sq_own = [w[:, :S] for w in bg_win], [w[:, S:] for w in bg_win]
-        a, root = [w[:, :S] for w in a_win], [w[:, S:] for w in a_win]
+        bg, under = [w[:, :S] for w in bg_win], [w[:, S:] for w in bg_win]
+        a, sq_g = [w[:, :S] for w in a_win], [w[:, S:] for w in a_win]
         for t in range(PACK):
             for cols, offsets in cut(n1_l):
                 nc.scalar.activation(tab_g[t][:, cols], tabs[t][:].indirect(offsets), ACT.Copy)
@@ -135,83 +132,93 @@ def tile_picked_pqjkindrmsratio_none_po_kernel(
             return banks
 
         b_gd = tile("b_gd", H, U8)
-        b_spread = after.tile([P, H + S], U8, name="b_spread", offset=4 * N - H, align_bytes=64)
-        b_gx = after.tile([P, S], U8, name="b_gx", offset=10 * N, align_bytes=64)
+        b_spread = after.tile([P, H + S], U8, name="b_spread", offset=S + 4 * N - H, align_bytes=64)
+        b_gx = after.tile([P, S], U8, name="b_gx", offset=0, align_bytes=64)
         b_xg = tile("b_xg", S, U32)
         b_dg = turns.tile([P, H], U32, name="b_dg", offset=0, align_bytes=64)
         b_banks = first_product("b", 0, k2_l, two_l, (b_gd[:], b_gx[:], b_xg[:], b_dg[:], b_spread))
-        gm_t = load_gain("gm_t", gm, 10 * N)
+        gm_t = load_gain("gm_t", gm, 0)
+        n4_l = load_list("n4_l", n4)
         a_bytes = turns.tile([P, H + S], U8, name="a_bytes", offset=0, align_bytes=64)
         a_words = turns.tile([P, S + H], U32, name="a_words", offset=H + S, align_bytes=64)
         a_banks = first_product("a", 1, k1_l, offs_l, (a_bytes[:, :H], a_bytes[:, H:], a_words[:, :S], a_words[:, S:], tile("a_spread", H + S, U8)))
 
-        w_raw = []
-        for l, src in enumerate((w1_words, w2_words)):
-            held = after.tile([P, N], U32, name=f"w_raw{l}", offset=l * 4 * N, align_bytes=64)
-            nc.sync.dma_start(held[:].bitcast(I32), src[0].rearrange("p c r -> p (c r)").bitcast(I32))
-            w_raw.append(held)
-        gn_t = load_gain("gn_t", gn, 10 * N + 64)
+        w_raw = [
+            load_words(after.tile([P, N], U32, name=f"w_raw{l}", offset=S + l * 4 * N, align_bytes=64), src)
+            for l, src in enumerate((w1_words, w2_words))
+        ]
+        gn_t = load_gain("gn_t", gn, 64)
+        n2_l = load_list("n2_l", n2)
+        n5_l = load_list("n5_l", n5)
+        n6_l = load_list("n6_l", n6)
         w_spread = turns.tile([P, 2 * N], U8, name="w_spread", offset=H + S, align_bytes=64)
         for l in range(2):
             deal(nc.vector.tensor_copy, w_spread[:, l * N : (l + 1) * N], w_bytes[:, l * N : (l + 1) * N], 16)
         for j in range(4):
             nc.sync.dma_start(w_scales[j:P:32, :].bitcast(I32), w_spread[8 * j : P : 32, :].bitcast(I32))
 
-        under, u, v, top = planes("under"), planes("u"), planes("v"), planes("top")
+        root, u, v, top = planes("root"), planes("u"), planes("v"), planes("top")
         z2 = tile("z2", PACK * S, F32)
         z = tile("z", PACK * S, BF16)
         for t in range(PACK):
             nc.scalar.activation(sq[t], b_banks[t][:], ACT.Square, scale=0.0625)
-            nc.scalar.activation(sq_own[t], b_banks[t][:], ACT.Square, scale=0.0625)
         for t in range(PACK):
-            nc.scalar.activation(bg[t], b_banks[t][:], ACT.Copy, scale=gm_t[:, t : t + 1])
-        for t in range(PACK):
-            nc.vector.tensor_tensor(under[t][:], sq_win[t][:].indirect(n3_l[:]), sq_own[t], ALU.add)
-        for t in range(PACK):
-            nc.scalar.activation(a[t], a_banks[t][:], ACT.Copy, scale=0.0625)
-        for t in range(PACK):
+            nc.scalar.activation(sq_g[t], sq_win[t][:].indirect(n3_l[:]), ACT.Copy)
+            nc.vector.tensor_tensor(under[t], sq[t], sq_g[t], ALU.add)
             nc.vector.scalar_tensor_tensor(u[t][:], a_banks[t][:], 0.0625, tab_g[t], ALU.mult, ALU.add)
         for t in range(PACK):
-            nc.scalar.activation(root[t], under[t][:], ACT.Abs_reciprocal_sqrt, bias=64.0, scale=256.0)
+            nc.scalar.activation(root[t][:], under[t], ACT.Abs_reciprocal_sqrt, bias=64.0, scale=256.0)
+            nc.scalar.activation(bg[t], b_banks[t][:], ACT.Copy, scale=gm_t[:, t : t + 1])
+            nc.vector.tensor_tensor(z2[:, t * S : (t + 1) * S], bg_win[t][:].indirect(n4_l[:]), root[t][:], ALU.mult)
         for t in range(PACK):
-            nc.vector.tensor_tensor(z2[:, t * S : (t + 1) * S], bg_win[t][:].indirect(n4_l[:]), root[t], ALU.mult)
-        for t in range(PACK):
+            nc.scalar.activation(a[t], a_banks[t][:], ACT.Copy, scale=0.0625)
             nc.scalar.activation(v[t][:], a_win[t][:].indirect(n2_l[:]), ACT.Copy)
-        w_words = []
-        for l in range(2):
-            held = sb.tile([P, N], U32, name=f"w_words{l}", tag=f"under{l + 2}", align_bytes=64)
-            deal(nc.scalar.copy, held[:], w_raw[l][:], 4)
-            w_words.append(held)
+        w_words = [
+            sb.tile([P, N], U32, name="w1_dealt", tag="a_win3", align_bytes=64),
+            sb.tile([P, N], U32, name="w2_dealt", tag="root3", align_bytes=64),
+        ]
+        deal(nc.scalar.copy, w_words[0][:], w_raw[0][:], 4)
+        deal(nc.vector.tensor_copy, w_words[1][:].bitcast(I32), w_raw[1][:].bitcast(I32), 4)
 
-        def quantise(name, src, scalar_cols):
-            grouped = tile(name + "_grouped", PACK * S, BF16)
+        def group(copy, grouped, src, lo, hi):
             dst = grouped[:].rearrange("p (c i t) -> p c t i", i=4, t=PACK)
             rows = src[:].rearrange("p (t c i) -> p c t i", i=4, t=PACK)
-            cut_at = scalar_cols // 4
-            if cut_at:
-                nc.scalar.copy(dst[:, :cut_at], rows[:, :cut_at])
-            nc.vector.tensor_copy(dst[:, cut_at:], rows[:, cut_at:])
-            words = tile(name + "_words", S, U32)
-            scales = tile(name + "_scales", S, U8)
-            nc.vector.quantize_mx(out=words[:].bitcast(FP8X4), scales=scales[:], in_=grouped[:])
-            return words, scales
+            copy(dst[:, lo // 4 : hi // 4], rows[:, lo // 4 : hi // 4])
 
-        for t in range(PACK):
-            nc.vector.tensor_tensor(top[t][:], u[t][:], v[t][:], ALU.max)
-        z2_q = quantise("z2", z2, 0)
-        for t in range(PACK):
-            nc.scalar.activation(z[:, t * S : (t + 1) * S], top[t][:], ACT.Copy, scale=gn_t[:, t : t + 1])
-        z_q = quantise("z", z, 256)
+        def mx_tiles(name):
+            return tile(name + "_grouped", PACK * S, BF16), tile(name + "_words", S, U32), tile(name + "_scales", S, U8)
 
-        h_banks = [psum.tile([P, S], F32, name=f"h{t}", tag=f"bank{t}") for t in range(PACK)]
-        for l, (words, scales) in ((1, z2_q), (0, z_q)):
-            for t in range(PACK):
+        def quantise(tiles, lo, hi):
+            grouped, words, scales = tiles
+            nc.vector.quantize_mx(out=words[:, lo:hi].bitcast(FP8X4), scales=scales[:, lo:hi], in_=grouped[:, PACK * lo : PACK * hi])
+
+        def quantise_shared(tiles, src):
+            group(nc.scalar.copy, tiles[0], src, S - SCALAR_COLS, S)
+            group(nc.vector.tensor_copy, tiles[0], src, 0, HALF)
+            group(nc.vector.tensor_copy, tiles[0], src, HALF, S - SCALAR_COLS)
+            quantise(tiles, 0, HALF)
+            quantise(tiles, HALF, S)
+
+        z2_q, z_q, y_q = mx_tiles("z2"), mx_tiles("z"), mx_tiles("y")
+        group(nc.vector.tensor_copy, z2_q[0], z2, 0, S)
+        nc.vector.tensor_tensor(top[0][:], u[0][:], v[0][:], ALU.max)
+        quantise(z2_q, 0, S)
+        for t in range(PACK):
+            if t + 1 < PACK:
+                nc.vector.tensor_tensor(top[t + 1][:], u[t + 1][:], v[t + 1][:], ALU.max)
+            nc.vector.tensor_scalar(z[:, t * S : (t + 1) * S], top[t][:], gn_t[:, t : t + 1], None, ALU.mult)
+        quantise_shared(z_q, z)
+
+        spans = [(0, 0, HALF, "bank0"), (0, HALF, S, "bank4")] + [(t, 0, S, f"bank{t}") for t in range(1, PACK)]
+        h_banks = [psum.tile([P, hi - lo], F32, name=f"h{t}_{lo}", tag=bank) for t, lo, hi, bank in spans]
+        for l, (grouped, words, scales) in ((1, z2_q), (0, z_q)):
+            for (t, lo, hi, bank), acc in zip(spans, h_banks):
                 nc.tensor.matmul_mx(
-                    out=h_banks[t][:],
+                    out=acc[:],
                     lhsT=w_words[l][:, t * P : (t + 1) * P].bitcast(FP8X4),
                     lhsT_scale=w_scales[:, l * N + t * P : l * N + (t + 1) * P],
-                    rhs=words[:].bitcast(FP8X4),
-                    rhs_scale=scales[:],
+                    rhs=words[:, lo:hi].bitcast(FP8X4),
+                    rhs_scale=scales[:, lo:hi],
                     start=(l == 1),
                     stop=(l == 0),
                 )
@@ -223,35 +230,53 @@ def tile_picked_pqjkindrmsratio_none_po_kernel(
         size_sq = [size_sq_all[:, t * W : (t + 1) * W] for t in range(PACK)]
         out_rows = out_0.rearrange("(p t) c -> p t c", t=PACK)
 
-        def fetch(t):
-            h = sb.tile([P, S], F32, name="h", tag=f"h{min(t, 1)}", align_bytes=64)
-            nc.scalar.activation(h[:], h_banks[t][:], ACT.Copy)
-            for dst, offsets in ((pb[t], n6_l), (pa[t], n5_l)):
-                if t == 0:
-                    nc.vector.tensor_copy(dst[:], h[:].indirect(offsets[:]))
-                else:
-                    nc.scalar.activation(dst[:], h[:].indirect(offsets[:]), ACT.Copy)
+        def empty_banks(plane):
+            h = sb.tile([P, S], F32, name="h", tag=f"h{min(plane, 1)}", align_bytes=64)
+            for (t, lo, hi, bank), acc in zip(spans, h_banks):
+                if t == plane:
+                    nc.scalar.activation(h[:, lo:hi], acc[:], ACT.Copy)
+            return h
+
+        def fetch(t, h):
+            if t == 0:
+                nc.vector.tensor_copy(pb[t][:], h[:].indirect(n6_l[:]))
+            else:
+                nc.scalar.activation(pb[t][:], h[:].indirect(n6_l[:]), ACT.Copy)
+            nc.scalar.activation(pa[t][:], h[:].indirect(n5_l[:]), ACT.Copy)
             nc.vector.tensor_tensor(rb[t][:], pa[t][:], pb[t][:], ALU.max)
 
-        fetch(0)
-        for t in range(PACK):
+        def put_larger(t):
             nc.vector.tensor_copy(y[t][:].indirect(n6_l[:]), rb[t][:])
-            if t + 1 < PACK:
-                fetch(t + 1)
+
+        def put_ratio(t):
             nc.scalar.activation(size[t][:], pb[t][:], ACT.Abs)
             nc.scalar.activation(size_sq[t], size[t][:], ACT.Square, bias=0.5)
             nc.scalar.activation(inverse[t][:], size_sq[t], ACT.Abs_reciprocal_sqrt)
             nc.vector.tensor_tensor(y[t][:].indirect(n5_l[:]), pa[t][:], inverse[t][:], ALU.mult)
             nc.sync.dma_start(out_rows[:, t, :], y[t][:])
-        y_bf = sb.tile([P, PACK * S], BF16, name="y_bf", tag="late", align_bytes=64)
-        for t in range(PACK):
-            if t < PACK - 1:
-                nc.scalar.copy(y_bf[:, t * S : (t + 1) * S], y[t][:])
-            else:
-                nc.vector.tensor_copy(y_bf[:, t * S : (t + 1) * S], y[t][:])
 
-        y_words, y_scales = quantise("y", y_bf, 128)
-        nc.sync.dma_start(out_1[0].rearrange("p c r -> p (c r)").bitcast(I32), y_words[:].bitcast(I32))
+        fetch(0, empty_banks(0))
+        put_larger(0)
+        put_ratio(0)
+        fetch(1, empty_banks(1))
+        for t in range(1, PACK):
+            put_larger(t)
+            if t + 1 < PACK:
+                fetch(t + 1, empty_banks(t + 1))
+            put_ratio(t)
+
+        y_bf = sb.tile([P, PACK * S], BF16, name="y_bf", tag="late", align_bytes=64)
+        last = PACK - 1
+        for t in range(last):
+            nc.scalar.copy(y_bf[:, t * S : (t + 1) * S], y[t][:])
+        for copy, lo, hi in ((nc.scalar.copy, S - SCALAR_COLS, S), (nc.vector.tensor_copy, 0, HALF), (nc.vector.tensor_copy, HALF, S - SCALAR_COLS)):
+            copy(y_bf[:, last * S + lo : last * S + hi], y[last][:, lo:hi])
+        quantise_shared(y_q, y_bf)
+
+        grouped, y_words, y_scales = y_q
+        words_out = out_1[0].rearrange("p c r -> p (c r)").bitcast(I32)
+        for lo, hi in ((0, HALF), (HALF, S)):
+            nc.sync.dma_start(words_out[:, lo:hi], y_words[:, lo:hi].bitcast(I32))
         for q in range(4):
             queue = nc.sync if q % 2 else nc.scalar
             queue.dma_start(out_2[0, 4 * q : 4 * q + 4, :].bitcast(I32), y_scales[32 * q : 32 * q + 4, :].bitcast(I32))

@@ -97,8 +97,8 @@ def tile_picked_pqjkindrmsratio_none_po_kernel(
 
         sq_win, bg_win, a_win = planes("sq_win", 2 * S), planes("bg_win", 2 * S), planes("a_win", 2 * S)
         sq, tab_g = [w[:, :S] for w in sq_win], [w[:, S:] for w in sq_win]
-        bg, under = [w[:, :S] for w in bg_win], [w[:, S:] for w in bg_win]
-        a, sq_g = [w[:, :S] for w in a_win], [w[:, S:] for w in a_win]
+        bg = [w[:, :S] for w in bg_win]
+        a, root = [w[:, :S] for w in a_win], [w[:, S:] for w in a_win]
         for t in range(PACK):
             for cols, offsets in cut(n1_l):
                 nc.scalar.activation(tab_g[t][:, cols], tabs[t][:].indirect(offsets), ACT.Copy)
@@ -157,25 +157,33 @@ def tile_picked_pqjkindrmsratio_none_po_kernel(
         for j in range(4):
             nc.sync.dma_start(w_scales[j:P:32, :].bitcast(I32), w_spread[8 * j : P : 32, :].bitcast(I32))
 
-        root, u, v, top = planes("root"), planes("u"), planes("v"), planes("top")
+        u, v, top = planes("u"), planes("v"), planes("top")
         z2 = tile("z2", PACK * S, F32)
         z = tile("z", PACK * S, BF16)
         for t in range(PACK):
             nc.scalar.activation(sq[t], b_banks[t][:], ACT.Square, scale=0.0625)
+        last = PACK - 1
+        under = [w[:, S:] for w in bg_win[:last]]
+        for t in range(last):
+            sq_g = tile(f"sq_g{t}", S, F32)
+            nc.scalar.activation(sq_g[:], sq_win[t][:].indirect(n3_l[:]), ACT.Copy)
+            nc.gpsimd.tensor_tensor(under[t], sq[t], sq_g[:], ALU.add)
+        nc.vector.tensor_copy(bg_win[last][:, S:], sq_win[last][:].indirect(n3_l[:]))
+        under_last = tile("under_last", S, F32)
+        nc.vector.tensor_tensor(under_last[:], sq[last], bg_win[last][:, S:], ALU.add)
+        under.append(under_last[:])
         for t in range(PACK):
-            nc.scalar.activation(sq_g[t], sq_win[t][:].indirect(n3_l[:]), ACT.Copy)
-            nc.vector.tensor_tensor(under[t], sq[t], sq_g[t], ALU.add)
             nc.vector.scalar_tensor_tensor(u[t][:], a_banks[t][:], 0.0625, tab_g[t], ALU.mult, ALU.add)
         for t in range(PACK):
-            nc.scalar.activation(root[t][:], under[t], ACT.Abs_reciprocal_sqrt, bias=64.0, scale=256.0)
+            nc.scalar.activation(root[t], under[t], ACT.Abs_reciprocal_sqrt, bias=64.0, scale=256.0)
             nc.scalar.activation(bg[t], b_banks[t][:], ACT.Copy, scale=gm_t[:, t : t + 1])
-            nc.vector.tensor_tensor(z2[:, t * S : (t + 1) * S], bg_win[t][:].indirect(n4_l[:]), root[t][:], ALU.mult)
+            nc.vector.tensor_tensor(z2[:, t * S : (t + 1) * S], bg_win[t][:].indirect(n4_l[:]), root[t], ALU.mult)
         for t in range(PACK):
             nc.scalar.activation(a[t], a_banks[t][:], ACT.Copy, scale=0.0625)
             nc.scalar.activation(v[t][:], a_win[t][:].indirect(n2_l[:]), ACT.Copy)
         w_words = [
             sb.tile([P, N], U32, name="w1_dealt", tag="a_win3", align_bytes=64),
-            sb.tile([P, N], U32, name="w2_dealt", tag="root3", align_bytes=64),
+            sb.tile([P, N], U32, name="w2_dealt", tag="bg_win3", align_bytes=64),
         ]
         deal(nc.scalar.copy, w_words[0][:], w_raw[0][:], 4)
         deal(nc.vector.tensor_copy, w_words[1][:].bitcast(I32), w_raw[1][:].bitcast(I32), 4)
@@ -266,7 +274,6 @@ def tile_picked_pqjkindrmsratio_none_po_kernel(
             put_ratio(t)
 
         y_bf = sb.tile([P, PACK * S], BF16, name="y_bf", tag="late", align_bytes=64)
-        last = PACK - 1
         for t in range(last):
             nc.scalar.copy(y_bf[:, t * S : (t + 1) * S], y[t][:])
         for copy, lo, hi in ((nc.scalar.copy, S - SCALAR_COLS, S), (nc.vector.tensor_copy, 0, HALF), (nc.vector.tensor_copy, HALF, S - SCALAR_COLS)):

from contextlib import ExitStack

import concourse.mybir as mybir

K, T, S, N, G, H, J, W = 512, 1024, 512, 512, 2048, 512, 512, 256
FLOPS = 4 * 2 * 512 * 512 * 512

F32 = mybir.dt.float32
BF16 = mybir.dt.bfloat16
I32 = mybir.dt.int32
U32 = mybir.dt.uint32
U16 = mybir.dt.uint16
U8 = mybir.dt.uint8
FP8X4 = mybir.dt.float8_e4m3fn_x4
ACT = mybir.ActivationFunctionType
ALU = mybir.AluOpType

P = 128
PACK = 4
HALF = S // 2
SCALAR_COLS = 128


def tile_picked_pqjkindrmsratio_none_po_kernel(
    tc, x_words, x_scales, d_words, d_scales, tab, gn, gm, w1_words, w1_scales, w2_words, w2_scales,
    offs, k1, two, k2, n1, n2, n3, n4, n5, n6, out_0, out_1, out_2,
):
    nc = tc.nc
    with ExitStack() as ctx:
        lists = ctx.enter_context(tc.tile_pool(name="lists", bufs=1))
        sb = ctx.enter_context(tc.tile_pool(name="sb", bufs=1))
        turns = ctx.enter_context(tc.tile_pool(name="turns", bufs=1))
        after = ctx.enter_context(tc.tile_pool(name="after", bufs=1))
        psum = ctx.enter_context(tc.psum_pool(name="psum", bufs=1))

        def tile(name, width, dtype):
            return sb.tile([P, width], dtype, name=name, align_bytes=64)

        def planes(name, width=S, dtype=F32):
            return [tile(f"{name}{t}", width, dtype) for t in range(PACK)]

        def load_list(name, src):
            held = lists.tile(list(src.shape), U16, name=name)
            nc.sync.dma_start(held[:], src)
            return held

        def load_words(held, src):
            nc.sync.dma_start(held[:].bitcast(I32), src[0].rearrange("p c r -> p (c r)").bitcast(I32))
            return held

        def cut(offsets):
            return [(slice(c * HALF, (c + 1) * HALF), offsets[:, c * HALF // 16 : (c + 1) * HALF // 16]) for c in range(2)]

        def deal(copy, dst, src, run):
            copy(dst.rearrange("p (t m i) -> p m t i", t=PACK, i=run), src.rearrange("p (m i t) -> p m t i", t=PACK, i=run))

        d_bytes = tile("d_bytes", G, U8)
        x_bytes = tile("x_bytes", T, U8)
        picked_scales = [tile("b_scales", H + S, U8), tile("a_scales", H + S, U8)]
        w_scales = tile("w_scales", 2 * N, U8)
        nc.gpsimd.memset(d_bytes[:].bitcast(I32), 0)
        nc.gpsimd.memset(x_bytes[:].bitcast(I32), 0)
        for held in picked_scales:
            nc.vector.memset(held[:].bitcast(I32), 0)
        nc.vector.memset(w_scales[:].bitcast(I32), 0)
        w_bytes = tile("w_bytes", 2 * N, U8)
        nc.vector.memset(w_bytes[:].bitcast(I32), 0)

        warm_in = sb.tile([P, 1], F32, name="warm_in")
        warm_out = sb.tile([P, 1], F32, name="warm_out")
        nc.vector.memset(warm_in[:], 1.0)
        nc.scalar.activation(warm_out[:], warm_in[:], ACT.Abs_reciprocal_sqrt)

        def load_gain(name, src, offset):
            held = after.tile([P, PACK], F32, name=name, offset=offset, align_bytes=64)
            nc.sync.dma_start(held[:], src.rearrange("(p t) o -> p (t o)", t=PACK))
            return held

        nc.sync.dma_start(d_bytes[0:P:8, :].bitcast(I32), d_scales[0].bitcast(I32))
        nc.sync.dma_start(x_bytes[0:P:8, :].bitcast(I32), x_scales[0].bitcast(I32))
        k2_l = load_list("k2_l", k2)
        two_l = load_list("two_l", two)
        n1_l = load_list("n1_l", n1)
        k1_l = load_list("k1_l", k1)
        tab_rows = tab.rearrange("(p t) c -> p t c", t=PACK)
        tabs = planes("tab")
        for t in range(2):
            nc.sync.dma_start(tabs[t][:], tab_rows[:, t, :])
        x_w = load_words(tile("x_w", T, U32), x_words)
        d_w = load_words(tile("d_w", G, U32), d_words)
        offs_l = load_list("offs_l", offs)
        for t in range(2, PACK):
            nc.sync.dma_start(tabs[t][:], tab_rows[:, t, :])
        n3_l = load_list("n3_l", n3)
        for l, src in enumerate((w1_scales, w2_scales)):
            nc.gpsimd.dma_start(w_bytes[0:P:8, l * N : (l + 1) * N].bitcast(I32), src[0].bitcast(I32))

        sq_win, bg_win, a_win = planes("sq_win", 2 * S), planes("bg_win", 2 * S), planes("a_win", 2 * S)
        sq, tab_g = [w[:, :S] for w in sq_win], [w[:, S:] for w in sq_win]
        bg = [w[:, :S] for w in bg_win]
        a, root = [w[:, :S] for w in a_win], [w[:, S:] for w in a_win]
        for t in range(PACK):
            for cols, offsets in cut(n1_l):
                nc.scalar.activation(tab_g[t][:, cols], tabs[t][:].indirect(offsets), ACT.Copy)

        def first_product(name, l, d_list, x_list, picked):
            gd, gx, xg, dg, spread = picked
            nc.vector.tensor_copy(gd, d_bytes[:].indirect(d_list[:]))
            nc.vector.tensor_copy(gx, x_bytes[:].indirect(x_list[:]))
            deal(nc.vector.tensor_copy, spread[:, :H], gd, 16)
            nc.vector.tensor_copy(spread[:, H:].bitcast(I32), gx.bitcast(I32))
            scales = picked_scales[l]
            for j in range(4):
                nc.sync.dma_start(scales[j:P:32, :].bitcast(I32), spread[8 * j : P : 32, :].bitcast(I32))
            nc.vector.tensor_copy(dg, d_w[:].indirect(d_list[:]))
            nc.vector.tensor_copy(xg, x_w[:].indirect(x_list[:]))
            dd = tile(name + "_dd", H, U32)
            deal(nc.vector.tensor_copy, dd[:].bitcast(I32), dg.bitcast(I32), 4)
            banks = []
            for t in range(PACK):
                bank = psum.tile([P, S], F32, name=f"{name}{t}", tag=f"bank{4 * l + t}")
                nc.tensor.matmul_mx(
                    out=bank[:],
                    lhsT=dd[:, t * P : (t + 1) * P].bitcast(FP8X4),
                    lhsT_scale=scales[:, t * P : (t + 1) * P],
                    rhs=xg.bitcast(FP8X4),
                    rhs_scale=scales[:, H:],
                    start=True,
                    stop=True,
                )
                banks.append(bank)
            return banks

        b_gd = tile("b_gd", H, U8)
        b_spread = after.tile([P, H + S], U8, name="b_spread", offset=S + 4 * N - H, align_bytes=64)
        b_gx = after.tile([P, S], U8, name="b_gx", offset=0, align_bytes=64)
        b_xg = tile("b_xg", S, U32)
        b_dg = turns.tile([P, H], U32, name="b_dg", offset=0, align_bytes=64)
        b_banks = first_product("b", 0, k2_l, two_l, (b_gd[:], b_gx[:], b_xg[:], b_dg[:], b_spread))
        gm_t = load_gain("gm_t", gm, 0)
        n4_l = load_list("n4_l", n4)
        a_bytes = turns.tile([P, H + S], U8, name="a_bytes", offset=0, align_bytes=64)
        a_words = turns.tile([P, S + H], U32, name="a_words", offset=H + S, align_bytes=64)
        a_banks = first_product("a", 1, k1_l, offs_l, (a_bytes[:, :H], a_bytes[:, H:], a_words[:, :S], a_words[:, S:], tile("a_spread", H + S, U8)))

        w_raw = [
            load_words(after.tile([P, N], U32, name=f"w_raw{l}", offset=S + l * 4 * N, align_bytes=64), src)
            for l, src in enumerate((w1_words, w2_words))
        ]
        gn_t = load_gain("gn_t", gn, 64)
        n2_l = load_list("n2_l", n2)
        n5_l = load_list("n5_l", n5)
        n6_l = load_list("n6_l", n6)
        w_spread = turns.tile([P, 2 * N], U8, name="w_spread", offset=H + S, align_bytes=64)
        for l in range(2):
            deal(nc.vector.tensor_copy, w_spread[:, l * N : (l + 1) * N], w_bytes[:, l * N : (l + 1) * N], 16)
        for j in range(4):
            nc.sync.dma_start(w_scales[j:P:32, :].bitcast(I32), w_spread[8 * j : P : 32, :].bitcast(I32))

        u, v, top = planes("u"), planes("v"), planes("top")
        z2 = tile("z2", PACK * S, F32)
        z = tile("z", PACK * S, BF16)
        for t in range(PACK):
            nc.scalar.activation(sq[t], b_banks[t][:], ACT.Square, scale=0.0625)
        last = PACK - 1
        under = [w[:, S:] for w in bg_win[:last]]
        for t in range(last):
            sq_g = tile(f"sq_g{t}", S, F32)
            nc.scalar.activation(sq_g[:], sq_win[t][:].indirect(n3_l[:]), ACT.Copy)
            nc.gpsimd.tensor_tensor(under[t], sq[t], sq_g[:], ALU.add)
        nc.vector.tensor_copy(bg_win[last][:, S:], sq_win[last][:].indirect(n3_l[:]))
        under_last = tile("under_last", S, F32)
        nc.vector.tensor_tensor(under_last[:], sq[last], bg_win[last][:, S:], ALU.add)
        under.append(under_last[:])
        for t in range(PACK):
            nc.vector.scalar_tensor_tensor(u[t][:], a_banks[t][:], 0.0625, tab_g[t], ALU.mult, ALU.add)
        for t in range(PACK):
            nc.scalar.activation(root[t], under[t], ACT.Abs_reciprocal_sqrt, bias=64.0, scale=256.0)
            nc.scalar.activation(bg[t], b_banks[t][:], ACT.Copy, scale=gm_t[:, t : t + 1])
            nc.vector.tensor_tensor(z2[:, t * S : (t + 1) * S], bg_win[t][:].indirect(n4_l[:]), root[t], ALU.mult)
        for t in range(PACK):
            nc.scalar.activation(a[t], a_banks[t][:], ACT.Copy, scale=0.0625)
            nc.scalar.activation(v[t][:], a_win[t][:].indirect(n2_l[:]), ACT.Copy)
        w_words = [
            sb.tile([P, N], U32, name="w1_dealt", tag="a_win3", align_bytes=64),
            sb.tile([P, N], U32, name="w2_dealt", tag="bg_win3", align_bytes=64),
        ]
        deal(nc.scalar.copy, w_words[0][:], w_raw[0][:], 4)
        deal(nc.vector.tensor_copy, w_words[1][:].bitcast(I32), w_raw[1][:].bitcast(I32), 4)

        def group(copy, grouped, src, lo, hi):
            dst = grouped[:].rearrange("p (c i t) -> p c t i", i=4, t=PACK)
            rows = src[:].rearrange("p (t c i) -> p c t i", i=4, t=PACK)
            copy(dst[:, lo // 4 : hi // 4], rows[:, lo // 4 : hi // 4])

        def mx_tiles(name):
            return tile(name + "_grouped", PACK * S, BF16), tile(name + "_words", S, U32), tile(name + "_scales", S, U8)

        def quantise(tiles, lo, hi):
            grouped, words, scales = tiles
            nc.vector.quantize_mx(out=words[:, lo:hi].bitcast(FP8X4), scales=scales[:, lo:hi], in_=grouped[:, PACK * lo : PACK * hi])

        def quantise_shared(tiles, src):
            group(nc.scalar.copy, tiles[0], src, S - SCALAR_COLS, S)
            group(nc.vector.tensor_copy, tiles[0], src, 0, HALF)
            group(nc.vector.tensor_copy, tiles[0], src, HALF, S - SCALAR_COLS)
            quantise(tiles, 0, HALF)
            quantise(tiles, HALF, S)

        z2_q, z_q, y_q = mx_tiles("z2"), mx_tiles("z"), mx_tiles("y")
        group(nc.vector.tensor_copy, z2_q[0], z2, 0, S)
        nc.vector.tensor_tensor(top[0][:], u[0][:], v[0][:], ALU.max)
        quantise(z2_q, 0, S)
        for t in range(PACK):
            if t + 1 < PACK:
                nc.vector.tensor_tensor(top[t + 1][:], u[t + 1][:], v[t + 1][:], ALU.max)
            nc.vector.tensor_scalar(z[:, t * S : (t + 1) * S], top[t][:], gn_t[:, t : t + 1], None, ALU.mult)
        quantise_shared(z_q, z)

        spans = [(0, 0, HALF, "bank0"), (0, HALF, S, "bank4")] + [(t, 0, S, f"bank{t}") for t in range(1, PACK)]
        h_banks = [psum.tile([P, hi - lo], F32, name=f"h{t}_{lo}", tag=bank) for t, lo, hi, bank in spans]
        for l, (grouped, words, scales) in ((1, z2_q), (0, z_q)):
            for (t, lo, hi, bank), acc in zip(spans, h_banks):
                nc.tensor.matmul_mx(
                    out=acc[:],
                    lhsT=w_words[l][:, t * P : (t + 1) * P].bitcast(FP8X4),
                    lhsT_scale=w_scales[:, l * N + t * P : l * N + (t + 1) * P],
                    rhs=words[:, lo:hi].bitcast(FP8X4),
                    rhs_scale=scales[:, lo:hi],
                    start=(l == 1),
                    stop=(l == 0),
                )

        y = planes("y")
        pa, pb, rb = planes("pa", W), planes("pb", W), planes("rb", W)
        size, inverse = planes("size", W), planes("inverse", W)
        size_sq_all = sb.tile([P, PACK * W], F32, name="size_sq_all", tag="late", align_bytes=64)
        size_sq = [size_sq_all[:, t * W : (t + 1) * W] for t in range(PACK)]
        out_rows = out_0.rearrange("(p t) c -> p t c", t=PACK)

        def empty_banks(plane):
            h = sb.tile([P, S], F32, name="h", tag=f"h{min(plane, 1)}", align_bytes=64)
            for (t, lo, hi, bank), acc in zip(spans, h_banks):
                if t == plane:
                    nc.scalar.activation(h[:, lo:hi], acc[:], ACT.Copy)
            return h

        def fetch(t, h):
            if t == 0:
                nc.vector.tensor_copy(pb[t][:], h[:].indirect(n6_l[:]))
            else:
                nc.scalar.activation(pb[t][:], h[:].indirect(n6_l[:]), ACT.Copy)
            nc.scalar.activation(pa[t][:], h[:].indirect(n5_l[:]), ACT.Copy)
            nc.vector.tensor_tensor(rb[t][:], pa[t][:], pb[t][:], ALU.max)

        def put_larger(t):
            nc.vector.tensor_copy(y[t][:].indirect(n6_l[:]), rb[t][:])

        def put_ratio(t):
            nc.scalar.activation(size[t][:], pb[t][:], ACT.Abs)
            nc.scalar.activation(size_sq[t], size[t][:], ACT.Square, bias=0.5)
            nc.scalar.activation(inverse[t][:], size_sq[t], ACT.Abs_reciprocal_sqrt)
            nc.vector.tensor_tensor(y[t][:].indirect(n5_l[:]), pa[t][:], inverse[t][:], ALU.mult)
            nc.sync.dma_start(out_rows[:, t, :], y[t][:])

        fetch(0, empty_banks(0))
        put_larger(0)
        put_ratio(0)
        fetch(1, empty_banks(1))
        for t in range(1, PACK):
            put_larger(t)
            if t + 1 < PACK:
                fetch(t + 1, empty_banks(t + 1))
            put_ratio(t)

        y_bf = sb.tile([P, PACK * S], BF16, name="y_bf", tag="late", align_bytes=64)
        for t in range(last):
            nc.scalar.copy(y_bf[:, t * S : (t + 1) * S], y[t][:])
        for copy, lo, hi in ((nc.scalar.copy, S - SCALAR_COLS, S), (nc.vector.tensor_copy, 0, HALF), (nc.vector.tensor_copy, HALF, S - SCALAR_COLS)):
            copy(y_bf[:, last * S + lo : last * S + hi], y[last][:, lo:hi])
        quantise_shared(y_q, y_bf)

        grouped, y_words, y_scales = y_q
        words_out = out_1[0].rearrange("p c r -> p (c r)").bitcast(I32)
        for lo, hi in ((0, HALF), (HALF, S)):
            nc.sync.dma_start(words_out[:, lo:hi], y_words[:, lo:hi].bitcast(I32))
        for q in range(4):
            queue = nc.sync if q % 2 else nc.scalar
            queue.dma_start(out_2[0, 4 * q : 4 * q + 4, :].bitcast(I32), y_scales[32 * q : 32 * q + 4, :].bitcast(I32))
